import numpy as np
import ml_dtypes


def mxq(x, axis, fmt="e4m3"):
    dtype, down = {"e4m3": (ml_dtypes.float8_e4m3fn, 7), "e5m2": (ml_dtypes.float8_e5m2, 14)}[fmt]
    v = np.moveaxis(np.asarray(x, np.float32).astype(ml_dtypes.bfloat16).astype(np.float64), axis, -1)
    blocks = v.reshape(v.shape[:-1] + (-1, 32))
    amax = np.abs(blocks).max(-1, keepdims=True)
    byte = np.maximum(np.where(amax > 0, np.frexp(amax)[1] - 1 + 127, 0) - down, 1)
    scale = np.exp2(byte - 127.0)
    codes = (blocks / scale).astype(np.float32).astype(dtype).astype(np.float64)
    return np.moveaxis((codes * scale).reshape(v.shape), -1, axis)


WIDE = False


def mx_kscale(k):
    if not WIDE:
        return np.ones(k)
    levels = np.array([10, -10, 5, -5, 0])
    if k % 512:
        return np.exp2(np.random.permutation(np.resize(levels, k // 32))).repeat(32)
    a = np.empty((k // 512, 16))
    for p in range(k // 512):
        a[p, :8] = np.random.permutation(np.resize(levels, 8))
        for g in range(8):
            far = levels[np.abs(levels - a[p, g]) >= 10]
            a[p, g + 8] = far[np.random.randint(len(far))]
    return np.exp2(a.ravel()).repeat(32)


BF16 = ml_dtypes.bfloat16


def bf(x):
    return np.asarray(x, np.float32).astype(BF16)


def f64(x):
    return np.asarray(x).astype(np.float64)


E2M1 = np.array([0.0, 0.5, 1.0, 1.5, 2.0, 3.0, 4.0, 6.0, -0.0, -0.5, -1.0, -1.5, -2.0, -3.0, -4.0, -6.0])


def pack_weight(w, fmt):
    k, n = w.shape
    w = f64(bf(w)).reshape(k // 32, 32, n)
    amax = np.abs(w).max(1)
    if fmt == "e4m3":
        byte = np.frexp(amax)[1] - 1 + 127 - 7
    else:
        mant, ex = np.frexp(amax / 6.0)
        byte = np.where(mant > 0.5, ex, ex - 1) + 127
    byte = np.clip(np.where(amax > 0, byte, 1), 1, 254)
    scaled = (w * np.exp2(127.0 - byte)[:, None, :]).reshape(k, n).astype(np.float32)
    by_word = np.ascontiguousarray(scaled.reshape(k // 512, 128, 4, n).transpose(0, 1, 3, 2))
    if fmt == "e4m3":
        words = by_word.astype(ml_dtypes.float8_e4m3fn).view(np.uint8)
    else:
        c = by_word.astype(ml_dtypes.float4_e2m1fn).view(np.uint8) & 0xF
        words = c[..., 0::2] | (c[..., 1::2] << 4)
    return np.ascontiguousarray(words), np.ascontiguousarray(byte.astype(np.uint8).reshape(k // 512, 16, n))


def unpack_weight(words, scales, fmt):
    g, p, n, _ = words.shape
    if fmt == "e4m3":
        vals = np.ascontiguousarray(words).view(ml_dtypes.float8_e4m3fn).astype(np.float64)
    else:
        nib = np.empty((g, p, n, 4), np.uint8)
        nib[..., 0::2] = words & 0xF
        nib[..., 1::2] = words >> 4
        vals = E2M1[nib]
    vals = vals * np.repeat(np.exp2(scales.astype(np.float64) - 127.0), 8, axis=1)[..., None]
    return vals.transpose(0, 1, 3, 2).reshape(g * 512, n)
def pack4(w):
    words, scales = pack_weight(w, "e2m1")
    return words.reshape(words.shape[0], 128, -1), scales


def unpack4(words, scales):
    return unpack_weight(words.reshape(words.shape[0], 128, -1, 2), scales, "e2m1")


P, T, F, H = 1024, 4, 512, 512


def setup_inputs():
    s, t = mx_kscale(P), mx_kscale(F)
    x = np.random.standard_normal((P, T, F)) * s[:, None, None] * t
    a = 0.5 * np.random.standard_normal((P, P)) / np.sqrt(P) / s[:, None] * s
    b = 0.35 * np.random.standard_normal((F, F)) / np.sqrt(F) / t[:, None] * t
    c = np.random.standard_normal((P, H)) / np.sqrt(H) / s[:, None]
    sc_words, sc_scales = pack4(a)
    fb_words, fb_scales = pack4(b)
    hs_words, hs_scales = pack4(c)
    return {"x": bf(x),
            "sc_words": sc_words, "sc_scales": sc_scales,
            "fb_words": fb_words, "fb_scales": fb_scales,
            "hs_words": hs_words, "hs_scales": hs_scales,
            "gain": bf(np.random.uniform(0.5, 1.5, F) / t)}


def reference(x, sc_words, sc_scales, fb_words, fb_scales, hs_words, hs_scales, gain):
    x, gain = f64(x), f64(gain)
    a = unpack4(sc_words, sc_scales)
    b = unpack4(fb_words, fb_scales)
    c = unpack4(hs_words, hs_scales)
    d = (a.T @ mxq(x, 0, "e4m3").reshape(P, T * F)).reshape(P, T, F)
    h1 = x + np.maximum(d, 0)
    e = (mxq(h1, 2, "e4m3").reshape(P * T, F) @ b).reshape(P, T, F)
    h2 = h1 + e
    q = mxq(h2, 0, "e4m3").reshape(P, T * F)
    to_left = (c[H:].T @ q[H:]).reshape(H, T, F)
    to_right = (c[:H].T @ q[:H]).reshape(H, T, F)
    return gain * to_left, gain * to_right

from contextlib import ExitStack

import concourse.mybir as mybir
from concourse.masks import make_identity

P, T, F, H = 1024, 4, 512, 512
FLOPS = 2 * P * P * T * F + 2 * P * T * F * F + 2 * 2 * H * H * T * F

F32 = mybir.dt.float32
BF16 = mybir.dt.bfloat16
U32 = mybir.dt.uint32
I32 = mybir.dt.int32
U8 = mybir.dt.uint8
FP8X4 = mybir.dt.float8_e4m3fn_x4
FP4X4 = mybir.dt.float4_e2m1fn_x4
ALU = mybir.AluOpType

NP = 128
LT, L2, L3 = 3, 8, 14
RUN = 2
Q1LAG = 1
XQ_AT = (4,7)
XCH = 4
SPLIT = 320
OE_V = (15,23,29,31)


def tile_parcel_band_hemisphere_coupling_t2_kernel(
    tc, x, sc_words, sc_scales, fb_words, fb_scales, hs_words, hs_scales, gain, out_left, out_right
):
    nc = tc.nc
    outs = (out_right, out_left)
    with ExitStack() as ctx:
        keep = ctx.enter_context(tc.tile_pool(name="keep", bufs=1))
        work = ctx.enter_context(tc.tile_pool(name="work", bufs=2))
        psum = ctx.enter_context(tc.psum_pool(name="psum", bufs=2))
        ctx.enter_context(tc.manual_schedule())

        ident = keep.tile([NP, NP], F32, name="ident")
        a_raw = keep.tile([NP, 2, 2 * P], U8, name="a_raw", align_bytes=64)
        a_sraw = keep.tile([NP, 2, P], U8, name="a_sraw", align_bytes=64)
        a_w = keep.tile([NP, 2, 2 * P], U8, name="a_w", align_bytes=64)
        a_s = keep.tile([NP, 2, P], U8, name="a_s", align_bytes=64)
        b_raw = keep.tile([NP, 2 * F], U8, name="b_raw", align_bytes=64)
        b_sraw = keep.tile([NP, F], U8, name="b_sraw", align_bytes=64)
        b_w = keep.tile([NP, 2 * F], U8, name="b_w", align_bytes=64)
        b_s = keep.tile([NP, F], U8, name="b_s", align_bytes=64)
        c_w = keep.tile([NP, 2, 2 * H], U8, name="c_w", align_bytes=64)
        c_s = keep.tile([NP, 2, H], U8, name="c_s", align_bytes=64)
        gain_b = keep.tile([NP, F], BF16, name="gain_b")
        xs = {}
        for w in range(T):
            for k in range(2):
                xt = keep.tile([NP, 4, F], BF16, name="x_%d_%d" % (w, k))
                xs[w, k] = xt

        nc.vector.memset(a_sraw[:].bitcast(I32), 0)
        nc.gpsimd.memset(b_sraw[:].bitcast(I32), 0)
        nc.gpsimd.memset(c_s[:].bitcast(I32), 0)
        make_identity(nc, ident[:])

        def load_x(w, k):
            nc.sync.dma_start(out=xs[w, k][:], in_=x[512 * k : 512 * k + 512, w, :].rearrange("(p t) f -> p t f", t=4))

        a_src = sc_words.bitcast(I32)
        def load_a(h):
            nc.sync.dma_start(
                out=a_raw[:].bitcast(I32)[:, :, 256 * h : 256 * h + 256],
                in_=a_src[:, :, 256 * h : 256 * h + 256].rearrange("g p n -> p g n"),
            )

        for q in range(4):
            nc.scalar.dma_start(
                out=a_sraw[32 * q : 32 * q + 4].bitcast(I32),
                in_=sc_scales.bitcast(I32)[:, 4 * q : 4 * q + 4, :].rearrange("g q n -> q g n"),
            )
        load_x(0, 0)
        load_a(0)
        load_x(0, 1)
        load_a(1)
        nc.sync.dma_start(out=b_raw[:].bitcast(I32), in_=fb_words.bitcast(I32)[0])
        for q in range(4):
            nc.sync.dma_start(
                out=b_sraw[32 * q : 32 * q + 4].bitcast(I32),
                in_=fb_scales.bitcast(I32)[0, 4 * q : 4 * q + 4, :],
            )
        load_x(1, 0)
        load_x(1, 1)
        nc.sync.dma_start(out=c_w[:].bitcast(I32), in_=hs_words.bitcast(I32).rearrange("g p n -> p g n"))
        for q in range(4):
            nc.sync.dma_start(
                out=c_s[32 * q : 32 * q + 4].bitcast(I32),
                in_=hs_scales.bitcast(I32)[:, 4 * q : 4 * q + 4, :].rearrange("g q n -> q g n"),
            )
        for w in (2, 3):
            for k in range(2):
                load_x(w, k)
        nc.sync.dma_start(out=gain_b[:], in_=gain.partition_broadcast(NP))

        def perm_a(h, k):
            nc.vector.tensor_copy(
                out=a_w[:, k, 1024 * h : 1024 * h + 1024].rearrange("p (t m b) -> p t m b", t=4, b=2),
                in_=a_raw[:, k, 1024 * h : 1024 * h + 1024].rearrange("p (m t b) -> p t m b", t=4, b=2),
            )
            nc.vector.tensor_copy(
                out=a_s[:, k, 512 * h : 512 * h + 512].rearrange("p (t m) -> p t m", t=4),
                in_=a_sraw[:, k, 512 * h : 512 * h + 512].rearrange("p (m t) -> p t m", t=4),
            )

        def perm_b():
            nc.vector.tensor_copy(
                out=b_w[:].rearrange("p (t m b) -> p t m b", t=4, b=2),
                in_=b_raw[:].rearrange("p (m t b) -> p t m b", t=4, b=2),
            )
            nc.vector.tensor_copy(
                out=b_s[:].rearrange("p (t m) -> p t m", t=4),
                in_=b_sraw[:].rearrange("p (m t) -> p t m", t=4),
            )

        xg, xc, xsc = {}, {}, {}

        def x_interleave(w, k, lo, hi, on_vector):
            if (w, k) not in xg:
                g = work.tile([NP, F, 4], BF16, name="xg_%d_%d" % (w, k), tag="xg", bufs=3, align_bytes=64)
                xg[w, k] = g
            dst = xg[w, k][:, lo:hi, :].rearrange("p (c i) t -> p c t i", i=4)
            src = xs[w, k][:, :, lo:hi].rearrange("p t (c i) -> p c t i", i=4)
            if on_vector:
                nc.vector.tensor_copy(out=dst, in_=src)
            else:
                nc.scalar.copy(out=dst, in_=src)

        def x_quantize(w, k):
            c = work.tile([NP, F], U32, name="xc_%d_%d" % (w, k), tag="xc", bufs=4, align_bytes=64)
            s = work.tile([NP, F], U8, name="xsc_%d_%d" % (w, k), tag="xsc", bufs=4, align_bytes=64)
            nc.vector.quantize_mx(out=c[:].bitcast(FP8X4), scales=s[:], in_=xg[w, k][:].rearrange("p f t -> p (f t)"))
            xc[w, k], xsc[w, k] = c, s

        d, h1, h1t, h1g, h1c, h1s, e, h2g, h2c, h2s, o = ({} for i in range(11))

        def mm1(i):
            u, t = divmod(i, 4)
            w, h = divmod(u, 2)
            acc = psum.tile([NP, F], F32, name="d_%d" % i, tag="d", bufs=2)
            for k in range(2):
                nc.tensor.matmul_mx(
                    out=acc[:],
                    lhsT=a_w[:, k, 1024 * h + 256 * t : 1024 * h + 256 * t + 256].bitcast(FP4X4),
                    lhsT_scale=a_s[:, k, 512 * h + 128 * t : 512 * h + 128 * t + 128],
                    rhs=xc[w, k][:].bitcast(FP8X4),
                    rhs_scale=xsc[w, k][:],
                    start=(k == 0),
                    stop=(k == 1),
                )
            d[i] = acc

        def add1(i):
            u, t = divmod(i, 4)
            w, h = divmod(u, 2)
            if t == 0:
                tile = work.tile([NP, 4, F], F32, name="h1_%d" % u, tag="h1", bufs=4)
                h1[u] = tile
            nc.vector.scalar_tensor_tensor(
                out=h1[u][:, t, :].rearrange("p (t m) -> p t m", t=4),
                in0=d[i][:].rearrange("p (m t) -> p t m", t=4),
                scalar=0.0,
                in1=xs[w, h][:, t, :].rearrange("p (m t) -> p t m", t=4),
                op0=ALU.max,
                op1=ALU.add,
            )

        def turn(i):
            u, t = divmod(i, 4)
            bank = psum.tile([NP, 4, NP], F32, name="h1t_%d" % i, tag="h1t", bufs=2)
            for b in range(4):
                nc.tensor.transpose(bank[:, b, :], h1[u][:, t, NP * b : NP * b + NP], ident[:])
            h1t[i] = bank

        def gather1(i):
            u, t = divmod(i, 4)
            if t == 0:
                tile = work.tile([NP, F, 4], BF16, name="h1g_%d" % u, tag="h1g", bufs=2, align_bytes=64)
                h1g[u] = tile
            nc.scalar.copy(
                out=h1g[u][:, NP * t : NP * t + NP, :],
                in_=h1t[i][:].rearrange("p t q -> p q t"),
            )

        def quant1(u):
            c = work.tile([NP, F], U32, name="h1c_%d" % u, tag="h1c", bufs=3, align_bytes=64)
            s = work.tile([NP, F], U8, name="h1s_%d" % u, tag="h1s", bufs=3, align_bytes=64)
            nc.vector.quantize_mx(out=c[:].bitcast(FP8X4), scales=s[:], in_=h1g[u][:].rearrange("p q t -> p (q t)"))
            h1c[u], h1s[u] = c, s

        def mm2(i):
            u, b = divmod(i, 4)
            bank = psum.tile([NP, 4, NP], F32, name="e_%d" % i, tag="e", bufs=2)
            for t in range(4):
                nc.tensor.matmul_mx(
                    out=bank[:, t, :],
                    lhsT=h1c[u][:, NP * t : NP * t + NP].bitcast(FP8X4),
                    lhsT_scale=h1s[u][:, NP * t : NP * t + NP],
                    rhs=b_w[:, 256 * b : 256 * b + 256].bitcast(FP4X4),
                    rhs_scale=b_s[:, NP * b : NP * b + NP],
                    start=True,
                    stop=True,
                )
            e[i] = bank

        def add2(i):
            u, b = divmod(i, 4)
            if b == 0:
                tile = work.tile([NP, F, 4], BF16, name="h2g_%d" % u, tag="h2g", bufs=2, align_bytes=64)
                h2g[u] = tile
            cols = slice(NP * b, NP * b + NP)
            nc.vector.tensor_tensor(
                out=h2g[u][:, cols, :].rearrange("p (a i) t -> p a t i", i=4),
                in0=e[i][:].rearrange("p t (a i) -> p a t i", i=4),
                in1=h1[u][:, :, cols].rearrange("p t (a i) -> p a t i", i=4),
                op=ALU.add,
            )

        def quant2(u):
            c = work.tile([NP, F], U32, name="h2c_%d" % u, tag="h2c", bufs=3, align_bytes=64)
            s = work.tile([NP, F], U8, name="h2s_%d" % u, tag="h2s", bufs=3, align_bytes=64)
            nc.vector.quantize_mx(out=c[:].bitcast(FP8X4), scales=s[:], in_=h2g[u][:].rearrange("p f t -> p (f t)"))
            h2c[u], h2s[u] = c, s

        def mm3(i):
            u, m = divmod(i, 4)
            g = u % 2
            bank = psum.tile([NP, F], F32, name="o_%d" % i, tag="o", bufs=2)
            nc.tensor.matmul_mx(
                out=bank[:],
                lhsT=c_w[:, g, 256 * m : 256 * m + 256].bitcast(FP4X4),
                lhsT_scale=c_s[:, g, NP * m : NP * m + NP],
                rhs=h2c[u][:].bitcast(FP8X4),
                rhs_scale=h2s[u][:],
                start=True,
                stop=True,
            )
            o[i] = bank

        def finish(i):
            u, m = divmod(i, 4)
            w, g = divmod(u, 2)
            res = work.tile([NP, F], F32, name="res_%d" % i, tag="res", bufs=6)
            if i in OE_V:
                nc.vector.tensor_tensor(
                    out=res[:].rearrange("p (m t) -> p m t", t=4),
                    in0=o[i][:].rearrange("p (t m) -> p m t", t=4),
                    in1=gain_b[:].rearrange("p (m t) -> p m t", t=4),
                    op=ALU.mult,
                )
            else:
                raw = work.tile([NP, F], F32, name="raw_%d" % i, tag="raw", bufs=4)
                nc.scalar.copy(
                    out=raw[:].rearrange("p (m t) -> p m t", t=4),
                    in_=o[i][:].rearrange("p (t m) -> p m t", t=4),
                )
                for part in range(2):
                    cols = slice(256 * part, 256 * part + 256)
                    nc.gpsimd.tensor_tensor(out=res[:, cols], in0=raw[:, cols], in1=gain_b[:, cols], op=ALU.mult)
            nc.sync.dma_start(out=outs[g][NP * m : NP * m + NP, w, :], in_=res[:])

        x_interleave(0, 0, 0, SPLIT, False)
        x_interleave(0, 1, 0, SPLIT, False)
        x_interleave(0, 0, SPLIT, F, True)
        perm_a(0, 0)
        x_quantize(0, 0)
        x_interleave(0, 1, SPLIT, F, True)
        perm_a(0, 1)
        x_quantize(0, 1)

        n = 32

        def ok(i):
            return 0 <= i < n

        for s in range(n + L3):
            i, j = s, s - LT
            w, r = s // 8 + 1, s % 8
            turns = [v for v in range(j - RUN + 1, j + 1) if ok(v)] if j % RUN == RUN - 1 else []
            for v in turns:
                turn(v)
            if ok(s - L3):
                mm3(s - L3)
            if ok(s - L2):
                mm2(s - L2)
            if ok(i):
                mm1(i)
            if s == 2:
                perm_a(1, 0)
                perm_a(1, 1)
            if s == 5:
                perm_b()
            if w < T:
                for c in range(2 * XCH):
                    if c * XQ_AT[1] // (2 * XCH) == r:
                        k, cc = divmod(c, XCH)
                        x_interleave(w, k, F // XCH * cc, F // XCH * (cc + 1), False)
            for v in turns:
                gather1(v)
            for u in range(8):
                if 4 * u + 3 + LT == s - Q1LAG:
                    quant1(u)
            if w < T:
                for k in range(2):
                    if XQ_AT[k] == r:
                        x_quantize(w, k)
            if ok(s - L2):
                add2(s - L2)
            if ok(i):
                add1(i)
            if ok(s - L2) and (s - L2) % 4 == 3:
                quant2((s - L2) // 4)
            if ok(s - L3):
                finish(s - L3)
